import numpy as np, ml_dtypes
CORES = [35,38,43,46]
N = 4
BF = ml_dtypes.bfloat16
def gentries(a):
    return np.ascontiguousarray(a.reshape(8, 16, -1).transpose(0, 2, 1)).reshape(8, -1)
def gtable(e):
    e = np.asarray(e); return np.ascontiguousarray(e.reshape(8, -1, 16).transpose(0, 2, 1)).reshape(128, -1).astype(np.int32)
W, M, H, SC, TH, CAP, RO = 4096, 256, 16, 16, 88, 64, 4
B = 8
LEV = np.arange(H).reshape(1, 1, H, 1)
def parts(rng):
    weak = rng.random((N, 8, 1, W)) < rng.choice(np.array([0.15, 0.3, 0.5]), (N, 8, 1, 1))
    size = np.where(weak, 0.25, rng.choice(np.array([0.5, 1.0]), (N, 8, 1, W)))
    s = (256 * size * rng.random((N, 8, 16, W))).astype(np.int64); w = rng.integers(0, 256, (N, 8, 16, W))
    c = rng.integers(0, W, (N, 8, H, M)); n = rng.integers(1, H + 1, (N, 8, M)); to = np.argsort(rng.random((N, 8, M)), axis=-1)
    return s, w, c, n, to
def pack(s, w, c, n, to):
    return {"st": s.reshape(N, 128, W).astype(np.float32).astype(BF), "wt": w.reshape(N, 128, W).astype(np.float32).astype(BF),
            "cs": np.stack([gtable(a.reshape(8, -1)) for a in c]), "ns": np.stack([gtable(a) for a in n]), "ds": np.stack([gtable(a) for a in to])}
def plant(rng, s, w, edge):
    k = 17 * B; pc = 1 + np.argsort(rng.random((N, 8, W - 1)), axis=-1)[..., :k]
    yes = (np.argsort(rng.random((N, 8, k, 16)), axis=-1) < np.repeat(np.arange(17), B)[:, None]).transpose(0, 1, 3, 2)
    ix = np.ascontiguousarray(np.broadcast_to(pc[:, :, None, :], (N, 8, 16, k)))
    if edge:
        a = rng.integers(1, 256 // SC, yes.shape); b = SC * a + yes
    else:
        a = np.where(yes, 0, 255); b = rng.integers(1, 256, yes.shape)
    np.put_along_axis(s, ix, a, 3); np.put_along_axis(w, ix, b, 3); s[..., 0] = 255
    return pc
def stacks(rng, pc, j):
    e = np.take_along_axis(pc, (j * B + rng.integers(0, B, j.shape)).reshape(N, 8, H * M), 2).reshape(j.shape)
    return np.where(LEV % 2 == 1, e, 0)
def setup_inputs(rng):
    return pack(*parts(rng))
def setup_inputs_room(rng):
    s, w, c, n, to = parts(rng); pc = plant(rng, s, w, False); n = rng.integers(2, H + 1, (N, 8, M))
    cnt = rng.permuted(np.tile(np.array([M, M // 2, M // 2, CAP + 1, CAP, CAP - 1, 1, 0]), (N, 1)), axis=1)
    pos = np.argsort(rng.random((N, 1, M)), axis=-1)
    top = np.where(pos < cnt[:, :, None], 16, 8)[:, :, None]
    kk = (1 + 2 * (rng.integers(0, H, (N, 8, M)) % (n // 2)))[:, :, None]
    j = np.where(LEV == kk, top, np.minimum(rng.integers(0, 17, (N, 8, H, M)), top))
    return pack(s, w, stacks(rng, pc, j), n, to)
def setup_inputs_ties(rng):
    s, w, c, n, to = parts(rng); pc = plant(rng, s, w, True)
    goal = TH - 1 + rng.integers(0, 3, (N, 1, M)); j = goal // 8 + (np.arange(8)[:, None] < goal % 8)
    e = rng.integers(0, min(15 - (TH + 1) // 8, (TH - 1) // 8) + 1, (N, 4, M))
    j = rng.permuted(np.concatenate([j[:, :4] + e, j[:, 4:] - e], axis=1), axis=1)
    m = np.arange(M); h = M // 2
    n = np.where(m < CAP // 4, rng.integers(4, H + 1, (N, 8, M)), np.where(m < h, 2, n))
    c = np.where(m < h, stacks(rng, pc, np.repeat(j[:, :, None], H, axis=2)), c)
    return pack(s, w, c, n, to)
def setup_inputs_alike(rng):
    s, w, c, n, to = parts(rng); half = rng.random((N, 1, M)) < 0.5
    n = np.where(half, rng.choice(np.array([1, 2, H - 1, H]), (N, 8, M)), n)
    c = np.where(half[:, :, None], rng.choice(np.array([0, 1, W // 2, W - 1]), (N, 8, H, M)), c)
    i = np.arange(M); to[:, 0] = i; to[:, 1] = i[::-1]; to[:, 2] = (i + 1) % M
    w[:, 3] = 255 * rng.integers(0, 2, (N, 16, W))
    return pack(s, w, c, n, to)
def setup_inputs_full(rng):
    s, w, c, n, to = parts(rng)
    n = np.where(rng.random((N, 8, M)) < 0.9, H - rng.integers(0, 2, (N, 8, M)), n)
    q = int(rng.integers(0, N)); a = (q + 1) % N; b = (q + int(rng.integers(2, N))) % N; g = rng.permutation(8)
    n[b, g[0]] = 1; s[q, g[1]] = 255
    n[a, g[1]] = H; c[a, g[1]] -= c[a, g[1]] % 2
    w[a, g[1], :, ::2] = 0; s[a, g[1], :, 1::2] = 0
    x = np.append(rng.permutation(M - 1)[:CAP - 1], M - 1); y = 1 + 2 * rng.integers(0, W // 2, (8, CAP))
    for k in range(8):
        c[a, k, 0, x] = 0; c[a, k, 1, x] = y[k]; n[a, k, x] = np.maximum(n[a, k, x], 2)
        sk = s[a, k]; wk = w[a, k]
        sk[:, y[k]] = 0; wk[:, y[k]] = np.maximum(wk[:, y[k]], 1)
    return pack(s, w, c, n, to)
def setup_inputs_spread(rng):
    s, w, c, n, to = parts(rng)
    s = (np.exp2(8 * rng.random((N, 8, 1, W))) * rng.random((N, 8, 16, W))).astype(np.int64)
    w = (np.exp2(8 * rng.random((N, 8, 1, W))) * rng.random((N, 8, 16, W))).astype(np.int64)
    return pack(s, w, c, n, to)
def check_inputs(d):
    bad = []
    for k in ("st", "wt"):
        a = np.asarray(d[k]).astype(np.float32)
        if not (np.all(a >= 0) and np.all(a <= 255) and np.all(a == np.floor(a))): bad.append("whole numbers of " + k)
    for k, lo, hi in (("cs", 0, W - 1), ("ns", 1, H), ("ds", 0, M - 1)):
        if np.min(d[k]) < lo or np.max(d[k]) > hi: bad.append("range of " + k)
    if np.any(np.sort(np.stack([gentries(a) for a in d["ds"]]), axis=-1) != np.arange(M)): bad.append("targets of a group differ")
    return bad
def reference(st, wt, cs, ns, ds):
    s = st.astype(np.float32).astype(np.int32).reshape(N, 8, 16, W); w = wt.astype(np.float32).astype(np.int32).reshape(N, 8, 16, W)
    c = np.stack([gentries(a) for a in cs]).astype(np.int64).reshape(N, 8, H, M); n = np.stack([gentries(a) for a in ns]).astype(np.int64)
    inv = np.argsort(np.stack([gentries(a) for a in ds]), axis=-1)
    imp = np.zeros((N, 8, 16, M), np.int64); site = np.arange(M)
    for t in range(RO):
        live = LEV < n[:, :, None]; c = np.where(live, c, 0)
        rho = np.take_along_axis(w, c.reshape(N, 8, 1, H * M), 3).reshape(N, 8, 16, H, M) * live[:, :, None]
        own = np.add.accumulate(rho[:, :, :, ::-1], axis=3)[:, :, :, ::-1]
        low = np.concatenate([c[:, :, :1], c[:, :, :-1]], axis=2)
        h = (((c * low) >> 5) + c + 77 * t) & (W - 1)
        over = own + imp[:, :, :, None] > SC * np.take_along_axis(s, h.reshape(N, 8, 1, H * M), 3).reshape(N, 8, 16, H, M)
        v = np.where(live & (LEV > 0), np.add.reduce(over.astype(np.int64), axis=2), 0)
        most = np.max(v, axis=2); ks = np.argmax(v, axis=2)
        c = np.where(live, (13 * c + 97 * v + t) & (W - 1), 0)
        ready = (most >= 9) & (np.add.reduce(most, axis=1, keepdims=True) >= TH); one = ready.astype(np.int64)
        slide = ready & (np.add.accumulate(one, axis=2) - one < CAP)
        load = np.take_along_axis(own, ks[:, :, None, None], 3)[:, :, :, 0]
        old = n; grow = ~slide & (old < H)
        top = np.take_along_axis(c, old[:, :, None] - 1, 2)[:, :, 0]
        e = np.where(grow[:, :, None] & (LEV == old[:, :, None]), ((31 * site + 997 * t + top) & (W - 1))[:, :, None], c)
        n = np.where(slide, ks, old + grow)
        nc, nn, ni = [], [], []
        for a in range(N):
            q = (a - 1 - t % (N - 1)) % N; i = inv[q]
            got = np.take_along_axis(slide[q], i, 1); k0 = np.take_along_axis(ks[q], i, 1); end = np.take_along_axis(old[q], i, 1)
            row = LEV[0] - n[a][:, None] + k0[:, None]
            run = np.take_along_axis(np.take_along_axis(c[q], i[:, None], 2), np.clip(row, 0, H - 1), 1)
            hit = got[:, None] & (row >= k0[:, None]) & (row < end[:, None])
            nc.append(np.where(hit, run, e[a])); nn.append(np.minimum(n[a] + got * (end - k0), H))
            ni.append(np.take_along_axis(load[q], i[:, None], 2) * got[:, None])
        c = np.stack(nc); n = np.stack(nn); imp = np.stack(ni)
    c = np.where(LEV < n[:, :, None], c, -1)
    return {"yc": np.stack([gtable(a.reshape(8, -1)) for a in c]).astype(np.float32), "yn": np.stack([gtable(a) for a in n]).astype(np.float32), "yi": imp.reshape(N, 128, M).astype(np.float32)}

from concourse.bass import DstId, RemoteDMATransfer
from concourse.mybir import dt, AluOpType, AxisListType, ActivationFunctionType

RO = 4
DEAD = 8448
f32, bf, f16, i32, u16 = "float32", "bfloat16", "float16", "int32", "uint16"


def sb(n, d):
    return ("sbuf", [128, n], d)


SCRATCH = {
    "wtab": sb(4112, bf), "sraw": sb(4096, bf), "stab": sb(8464, bf),
    "csi": sb(256, i32), "nsi": sb(16, i32), "dsi": sb(16, i32),
    "wg": sb(4096, bf), "own": sb(4096, f16), "d0": sb(4096, f16), "over": sb(4096, bf), "sgo": sb(1024, bf),
    "c": sb(256, f32), "comb": sb(256, f32), "cu": sb(256, u16), "hu": sb(256, u16),
    "ia": sb(256, i32), "ib": sb(256, i32), "fa": sb(256, f32), "fb": sb(256, f32), "fc": sb(256, f32), "ha": sb(256, f16),
    "sg": sb(256, bf), "top": sb(256, f32), "vb": sb(256, bf), "pc": sb(256, f32), "mm": sb(256, f32), "loc": sb(256, f32),
    "ks": sb(256, f16), "kt": sb(256, f32), "cw": sb(512, f32), "rw": sb(1032, f32), "rsx": sb(256, f32), "lg": sb(1024, bf),
    "yis": sb(256, f32), "ycs": sb(256, f32), "yns": sb(16, f32), "ivb": sb(256, bf),
    "tb": sb(80, bf), "tf": sb(128, f32), "tu": sb(96, u16), "ti": sb(48, i32), "ci": sb(256, i32), "cf": sb(64, f32), "lu": sb(64, u16),
    "smeta": sb(64, u16), "rmeta": sb(64, u16), "spay": sb(256, f16), "rpay": sb(256, f16), "sload": sb(256, f32), "rload": sb(288, f32),
    "sinv": sb(16, u16), "rinv": sb(64, u16),
    "jf": sb(128, f32), "ji": sb(128, i32), "pi": sb(16, i32), "pf": sb(32, f32), "io16": sb(272, f32), "sio": sb(256, f32), "g8": sb(128, f32),
    "rb": sb(128, bf), "rot": sb(2048, f16), "sel": sb(144, bf), "sel8": sb(144, bf), "sh": sb(128, f32), "topm": sb(128, bf),
    "idf": sb(256, f32), "idb": sb(640, bf), "sw": sb(512, f16), "sumg": sb(128, bf), "bd": sb(256, bf), "t1": sb(256, bf),
    "mtab": sb(272, f32), "dtab": sb(32, f32), "ktab": sb(32, f32), "xtab": sb(1032, f32), "diag": sb(256, f32), "rst": sb(256, f32),
    "ck": sb(128, bf), "ce": sb(256, f32), "oc": sb(16, f32), "pl": sb(64, f32), "plu": sb(32, u16), "c2k": sb(256, bf),
}
for _k in range(8):
    SCRATCH["p%d" % _k] = ("psum", [128, 512], f32)

SEMAPHORES = ["qv", "qs", "qt", "qg", "ls", "ainv", "dcs", "dns", "dds", "dw0", "dw1", "ds0", "ds1", "ds2", "ds3", "oc", "on", "oi"] + \
    ["am%d" % t for t in range(RO)] + ["ap%d" % t for t in range(RO)] + ["al%d" % t for t in range(RO)]

A = AluOpType
F = ActivationFunctionType


def emit(g, T, ops):
    queue = {"v": g.vector, "s": g.scalar, "t": g.tensor, "g": g, "y": g.sync}
    qsem = {"v": "qv", "s": "qs", "t": "qt", "g": "qg"}
    wr, rd, deps, need = {}, {}, [], set()
    for n, (q, fn, r, w, sem, ext) in enumerate(ops):
        d = set()
        for k in r:
            if k in wr:
                d.add(wr[k])
            if k[0] == "#":
                d.update(m for m in rd.get(k, []) if ops[m][0] != q)
        for k in w:
            if k in wr:
                d.add(wr[k])
            d.update(rd.get(k, []))
        d = set(m for m in d if not (q == "t" and ops[m][0] == "t"))
        for k in r:
            rd.setdefault(k, []).append(n)
        for k in w:
            wr[k] = n
            rd[k] = []
        last = {}
        for m in d:
            key = ops[m][4] or ops[m][0]
            last[key] = max(last.get(key, -1), m)
        deps.append(sorted(last.values()))
    seen = {}
    for n, d in enumerate(deps):
        keep = []
        for m in d:
            key = (ops[n][0], ops[m][4] or ops[m][0])
            if seen.get(key, -1) < m:
                seen[key] = m
                keep.append(m)
        deps[n] = keep
        need.update(keep)
    count, at, waited = {}, {}, {}
    for n, (q, fn, r, w, sem, ext) in enumerate(ops):
        for s, v in ext:
            if waited.get((q, s), 0) < v:
                queue[q].wait_ge(T.sem[s], v)
                waited[(q, s)] = v
        for m in deps[n]:
            s, v = at[m]
            queue[q].wait_ge(T.sem[s], v)
        ins = fn()
        if sem:
            count[sem] = count.get(sem, 0) + 16
            ins.then_inc(T.sem[sem], 16)
            at[n] = (sem, count[sem])
        elif n in need:
            s = qsem[q]
            count[s] = count.get(s, 0) + 1
            ins.then_inc(T.sem[s], 1)
            at[n] = (s, count[s])
    return count


def rank_program(g, core, T, topo):
    rank = T.rank_of(core)
    if rank is None:
        return
    cores = list(T.cores)
    N = len(cores)
    ops = []
    V, S, PE = g.vector, g.scalar, g.tensor

    def op(q, fn, r, w, sem=None, ext=()):
        ops.append((q, fn, list(r), list(w), sem, list(ext)))

    def ts(out, in0, s1, o0, r, w, s2=None, o1=None, ext=()):
        if o1 is None:
            op("v", lambda: V.tensor_scalar(out, in0, s1, None, o0), r, w, None, ext)
        else:
            op("v", lambda: V.tensor_scalar(out, in0, s1, s2, o0, o1), r, w, None, ext)

    def tt(out, a, b, o, r, w, ext=()):
        op("v", lambda: V.tensor_tensor(out, a, b, o), r, w, None, ext)

    def cp(out, a, r, w, ext=()):
        op("v", lambda: V.tensor_copy(out, a), r, w, None, ext)

    def ms(out, v, w):
        op("v", lambda: V.memset(out, v), [], w)

    def scan(out, a, b, init, o0, o1, r, w):
        op("v", lambda: V.tensor_tensor_scan(out, a, b, init, o0, o1), r, w)

    def act(out, a, f, r, w, bias=0.0, scale=1.0, ext=()):
        op("s", lambda: S.activation(out, a, f, bias=bias, scale=scale), r, w, None, ext)

    def mm(out, l, rh, st, sp, r, w, ext=()):
        op("t", lambda: PE.matmul(out, l, rh, st, sp), r, w, None, ext)

    def iota(out, pat, base, cm, w, flt=True):
        if flt:
            op("g", lambda: g.iota(out, pat, base, cm, allow_small_or_imprecise_dtypes=True), [], w)
        else:
            op("g", lambda: g.iota(out, pat, base, cm), [], w)

    def pick(out, a, pat, cmp, fill, base, cm, r, w):
        op("g", lambda: g.affine_select(out, a, pat, cmp, fill, base, cm), [r], [w])

    def dma(out, a, r, w, sem, q="y"):
        op(q, lambda: (g.sync if q == "y" else S).dma_start(out, a), r, w, sem)

    sent = [0]

    def send(dst_rank, out, a, sem, r):
        dst = cores[dst_rank]
        rid, pid = topo.addr(dst)[:2]
        sent[0] += len(topo.engines(core, dst))
        op("g", lambda: g.remote_dma(out, a, T.sem[sem], T.sem.ls, pid, rid, topo.mask(core, dst)), r, [])

    def arrives(src_rank):
        return len(topo.engines(cores[src_rank], core))

    P = [T["p%d" % k] for k in range(8)]
    pf, pi = T.pf, T.pi
    RHO, GC, B0, B1, RT, KC, K8, CCOL, KAP, U32 = [pf[:, j:j + 1] for j in range(10)]
    HC = [pf[:, 10 + t:11 + t] for t in range(RO)]
    EPS, G16, NRHO = pf[:, 14:15], pf[:, 15:16], pf[:, 16:17]
    IDF, ID13 = T.idf[:, 0:128], T.idf[:, 128:256]
    IB, IB97, IBV, IB256, IBM16 = [T.idb[:, 128 * j:128 * j + 128] for j in range(5)]
    SEL = [T.sel[:, 16 - r:144 - r] for r in range(16)]
    SEL8 = [T.sel8[:, 16 - r:144 - r] for r in range(16)]
    WT = ["w0", "w1", "w2"]
    ST = ["s0", "s1", "s2", "s3", "s4", "u0", "u1", "u2", "u3", "u4"]
    C = ["c0", "c1"]

    dma(T.csi[:], T.cs[:], [], ["csi"], "dcs")
    dma(T.nsi[:], T.ns[:], [], ["nsi"], "dns", "s")
    dma(T.dsi[:], T.ds[:], [], ["dsi"], "dds", "s")
    dma(T.wtab[:, 0:2048], T.wt[:, 0:2048], [], ["w0"], "dw0")
    dma(T.wtab[:, 2048:4096], T.wt[:, 2048:4096], [], ["w1"], "dw1")
    for j in range(4):
        dma(T.sraw[:, 1024 * j:1024 * j + 1024], T.st[:, 1024 * j:1024 * j + 1024], [], ["sr%d" % j], "ds%d" % j)

    iota(pi[:, 0:1], [[0, 1]], 0, 1, ["pi0"], False)
    iota(T.jf[:], [[1, 128]], 0, -1, ["jf"])
    iota(T.pl[:, 0:16], [[1, 8], [128, 2]], 0, 0, ["pl0"])
    iota(T.sio[:], [[1, 256]], 0, 0, ["sio"])
    iota(T.ji[:], [[1, 128]], 128, -1, ["ji"], False)
    iota(T.g8[:], [[1, 8], [0, 16]], 0, 0, ["g8"])
    iota(T.io16[:], [[0, 17], [1, 16]], 0, 0, ["io16"])
    iota(T.oc[:], [[16, 16]], -255, 0, ["oc"])
    iota(T.pl[:, 16:32], [[0, 2], [-2, 8]], 16, 0, ["pl1"])
    iota(T.pl[:, 32:48], [[16, 2], [0, 8]], 0, 0, ["pl2"])
    ms(T.d0[:, 0:3072], 30000.0, ["d0"])
    ms(T.bd[:, 0:128], 1.0, ["bd0"])
    pick(T.bd[:, 0:128], T.bd[:, 0:128], [[-16, 8], [0, 16]], A.is_ge, 0.0, 0, 1, "bd0", "bd0")
    pick(T.bd[:, 0:128], T.bd[:, 0:128], [[16, 8], [0, 16]], A.is_ge, 0.0, 15, -1, "bd0", "bd0")
    pick(T.topm[:], T.bd[:, 0:128], [[-1, 128]], A.is_gt, 0.0, 0, 1, "bd0", "topm")
    pick(T.topm[:], T.topm[:], [[-1, 128]], A.not_equal, 512.0, 0, 1, "topm", "topm")
    iota(T.xtab[:, 0:1024], [[1, 64], [64, 16]], 0, 0, ["xtab"])
    ts(pi[:, 1:2], pi[:, 0:1], 15, A.bitwise_and, ["pi0"], ["pi1"])
    ts(pi[:, 2:3], pi[:, 0:1], 4, A.logical_shift_right, ["pi0"], ["pi2"])
    ts(pi[:, 3:4], pi[:, 0:1], 4, A.logical_shift_right, ["pi0"], ["pi3"], 1, A.bitwise_and)
    ms(T.wtab[:, 4096:4112], 0.0, ["w2"])
    cp(RHO, pi[:, 1:2], ["pi1"], ["RHO"])
    cp(B1, pi[:, 3:4], ["pi3"], ["B1"])
    ts(B0, pi[:, 3:4], -1.0, A.mult, ["pi3"], ["B0"], 1.0, A.add)
    ts(CCOL, pi[:, 1:2], 0.0, A.is_equal, ["pi1"], ["CCOL"], 4097.0, A.mult)
    ts(RT, pi[:, 1:2], 0.0, A.is_equal, ["pi1"], ["RT"], 16.0, A.mult)
    cp(GC, pi[:, 2:3], ["pi2"], ["GC"])
    ts(G16, pi[:, 2:3], 16.0, A.mult, ["pi2"], ["G16"], 16.0, A.add)
    ts(T.ha[:], T.csi[:], -2048.0, A.add, ["csi"], ["ha"])
    for b in range(2):
        for e in range(2):
            j = 2 * b + e
            ts(T.sw[:, 128 * j:128 * j + 128], T.jf[:], float(16 * (e - b)), A.is_equal, ["jf", "B0", "B1"], ["sw%d" % j], B1 if b else B0, A.mult)
    for b in range(2):
        for e in range(2):
            j = 2 * b + e
            mm(P[5][:, 128 * b:128 * b + 128], T.sw[:, 128 * j:128 * j + 128], T.ha[:, e::2], e == 0, e == 1, ["sw%d" % j, "ha"], ["#5"])
    ts(RT, RT, RHO, A.add, ["RT", "RHO"], ["RT"])
    ts(IDF, T.jf[:], 0.0, A.is_equal, ["jf"], ["idf"])
    ts(K8, RT, -8.0, A.mult, ["RT"], ["K8"], 128.0, A.add)
    ts(KC, RT, -1.0, A.mult, ["RT"], ["KC"], 16.0, A.add)
    act(T.fa[:], P[5][:, 0:256], F.Copy, ["#5"], ["fa"], bias=2048.0)
    ts(T.plu[:, 0:16], T.pl[:, 0:16], K8, A.add, ["pl0", "K8"], ["plu0"])
    cp(T.tu[:, 0:16], T.nsi[:], ["nsi"], ["nu"])
    ts(T.dtab[:], T.sio[:, 0:32], KC, A.is_le, ["sio", "KC"], ["dtab"], float(DEAD), A.mult)
    cp(T.fb[:], T.fa[:].indirect(T.plu[:, 0:16]), ["fa", "plu0"], ["fb"])
    ts(T.ji[:], T.ji[:], 15, A.bitwise_and, ["ji"], ["ji"])
    op("v", lambda: V.transpose(T.fc[:], T.fb[:]), ["fb"], ["fc"])
    ts(T.ycs[:, 0:128], T.g8[:], GC, A.not_equal, ["g8", "GC"], ["ycs"], 100.0, A.mult)
    tt(T.c[:], T.dtab[:].indirect(T.tu[:, 0:16]), T.fc[:], A.max, ["dtab", "nu", "fc"], C)
    tt(T.rb[:], T.ycs[:, 0:128], T.ji[:], A.add, ["ycs", "ji"], ["rb"])
    ms(T.wtab[:, 4097:4098], 16384.0, ["w2"])
    ts(T.sh[:], T.rb[:], 15.0, A.is_equal, ["rb"], ["sh"])
    for t in range(RO):
        ts(HC[t], CCOL, 3.0, A.mult, ["CCOL"], ["HC%d" % t], float(77 * t), A.add)
    for j, v in enumerate([1.0, 97.0, 131072.0, 256.0, -16.0]):
        act(T.idb[:, 128 * j:128 * j + 128], IDF, F.Copy, ["idf"], ["idb%d" % j], scale=v)
    act(ID13, IDF, F.Copy, ["idf"], ["id13"], scale=13.0)

    def growth(t):
        act(T.ce[:], T.sio[:], F.Copy, ["sio"], ["ce"], scale=31.0, bias=float(997 * t + (-13 * DEAD) % 4096))

    growth(0)
    act(T.t1[:, 0:128], T.topm[:], F.Copy, ["topm"], ["t1a"], scale=-1.0)
    act(T.t1[:, 128:256], T.topm[:], F.Copy, ["topm"], ["t1b"], scale=-16.0)
    act(T.bd[:, 128:256], T.bd[:, 0:128], F.Copy, ["bd0"], ["bd1"], scale=16.0)

    def consts_wide():
        ms(T.d0[:, 1:1024:16], -128.0, ["d0"])
        ts(T.sel[:], T.sio[:, 0:144], G16, A.is_equal, ["sio", "G16"], ["sel"], 16.0, A.mult)
        ts(T.sel8[:], T.sio[:, 0:144], G16, A.is_equal, ["sio", "G16"], ["sel8"], 8.0, A.mult)
        ms(T.stab[:, 8448:8464], 30000.0, ["s4"])
        ts(T.ck[:, 0:64], T.sio[:, 0:64], 0.0, A.mult, ["sio", "RHO"], ["ck0"], RHO, A.add)
        ts(NRHO, RHO, -0.0625, A.mult, ["RHO"], ["NRHO"])
        ts(T.ck[:, 64:128], T.ck[:, 0:64], 128.0, A.add, ["ck0"], ["ck1"])
        ms(EPS, -0.03125, ["EPS"])
        ts(T.rot[:, 0:128], IDF, -1.0, A.mult, ["idf"], ["rot0"])

    def consts_inv():
        cp(T.tu[:, 80:96], T.dsi[:], ["dsi"], ["du"])
        ts(T.rst[:], T.io16[:, 0:256], 0.0, A.not_equal, ["io16"], ["rst"])
        cp(T.ivb[:].indirect(T.tu[:, 80:96]), T.sio[:], ["du", "sio"], ["ivb"])
        for r in range(16):
            mm(P[4][:, 80:96], SEL[r], T.ivb[:, r::16], r == 0, r == 15, ["sel", "ivb"], ["#4"])
        ts(T.diag[:], T.io16[:, 0:256], RHO, A.is_equal, ["io16", "RHO"], ["diag"])
        ts(T.sinv[:], P[4][:, 80:96], 1.0 / 256, A.mult, ["#4"], ["sinv"])
        for d in range(1, N):
            send((rank + d) % N, T.rinv[:, 16 * d:16 * d + 16], T.sinv[:], "ainv", ["sinv"])

    def consts_tail():
        ts(T.sumg[:], T.ji[:], 0.0, A.is_equal, ["ji"], ["sumg"])
        ts(T.mtab[:], T.io16[:], RT, A.is_lt, ["io16", "RT"], ["mtab"], 4194304.0, A.mult)
        ts(T.oc[:], T.oc[:], RHO, A.add, ["oc", "RHO"], ["oc"])
        ts(T.ycs[:, 128:256], T.rb[:], 1.0, A.is_equal, ["rb"], ["ycs2"])
        ts(T.ktab[:], T.dtab[:], -3.0, A.mult, ["dtab"], ["ktab"], float(2 * DEAD), A.add)
        tt(T.topm[:], T.ycs[:, 128:256], IDF, A.subtract, ["ycs2", "idf"], ["topm"])
        ms(T.cw[:, 0:64], 0.0, ["cw"])

    def consts_land():
        ms(T.xtab[:, 1024:1032], 4096.0, ["xt2"])
        ms(T.rw[:, 1024:1032], float(-DEAD), ["rw2"])
        for x in range(1, 16):
            ts(T.rot[:, 128 * x:128 * x + 128], T.rb[:], float(16 - x), A.is_equal, ["rb"], ["rot%d" % x], -1.0, A.mult)
        for u in range(RO):
            ms(T.rload[:, 72 * u + 64:72 * u + 72], 0.0, ["rl%d" % u])

    def consts_end():
        ts(pi[:, 4:5], pi[:, 0:1], 3, A.logical_shift_right, ["pi0"], ["pi4"], 1, A.bitwise_and)
        ts(pi[:, 5:6], pi[:, 0:1], 7, A.bitwise_and, ["pi0"], ["pi5"])
        ms(T.c2k[:], 8.0, ["c2k"])
        cp(KAP, pi[:, 4:5], ["pi4"], ["KAP"])
        ts(U32, pi[:, 5:6], 32.0, A.mult, ["pi5"], ["U32"])
        ts(T.ti[:, 0:16], T.pl[:, 16:32], KAP, A.subtract, ["pl1", "KAP"], ["ti0"])
        ts(T.pl[:, 32:48], T.pl[:, 32:48], U32, A.add, ["pl2", "U32"], ["pl2"])
        ts(T.ti[:, 0:16], T.ti[:, 0:16], 15, A.bitwise_and, ["ti0"], ["ti0"])
        tt(T.pl[:, 48:64], T.ti[:, 0:16], T.pl[:, 32:48], A.add, ["ti0", "pl2"], ["pl3"])
        cp(T.plu[:, 16:32], T.pl[:, 48:64], ["pl3"], ["plu1"])

    def strengths(j):
        a, b = 1024 * j, 1024 * j + 1024
        ts(T.stab[:, a:b], T.sraw[:, a:b], -128.0, A.add, ["sr%d" % j], ["s%d" % j])
        if j == 0:
            ts(T.stab[:, 8192:8448], T.sraw[:, 0:256], -128.0, A.add, ["sr0"], ["u4"])

    def strengths_up(j):
        a, b = 1024 * j, 1024 * j + 1024
        act(T.stab[:, 4096 + a:4096 + b], T.sraw[:, a:b], F.Copy, ["sr%d" % j], ["u%d" % j], bias=-128.0)

    MP, T9, RDY, CUM, KS = [T.tb[:, 16 * j:16 * j + 16] for j in range(5)]
    AN, OF, NS, KB, NP, N64 = [T.tf[:, 16 * j:16 * j + 16] for j in range(6)]
    KU, OU, NU, RO_U, SL_U = [T.tu[:, 16 * j:16 * j + 16] for j in range(5)]
    OV = [["ov%d" % (2 * q + u) for u in range(2)] for q in range(4)]

    def gather_w(q):
        a, b = 1024 * q, 1024 * q + 1024
        act(T.wg[:, a:b], T.wtab[:].indirect(T.cu[:, 64 * q:64 * q + 64]), F.Copy, WT + ["cu%d" % min(q, 1)], ["wg%d" % q], scale=0.0625)

    def do_scan(q, t):
        a, b = 1024 * q, 1024 * q + 1024
        d0 = T.d0[:, a:b] if t else T.d0[:, 0:1024]
        scan(T.own[:, a:b], d0, T.wg[:, a:b], 0.0, A.min, A.add, ["d0", "wg%d" % q], ["own%d" % q])

    def votes(q):
        sel, nm, ck = (SEL, "sel", T.ck[:, 0:64]) if q < 3 else (SEL8, "sel8", T.ck[:, 64:128])
        k = 1 if q == 2 else 0
        o = P[k][:, 64 * q:64 * q + 64]
        mm(o, IB, ck, True, False, ["idb0", "ck0", "ck1"], ["#%d" % k])
        for r in range(0 if q == 3 else 1, 16):
            mm(o, sel[r], T.over[:, 1024 * q + r:1024 * q + 1024:16], False, r == 15, [nm] + OV[q], ["#%d" % k])

    def compare(q, a=0, b=2):
        lo, hi = 512 * (2 * q + a), 512 * (2 * q + b)
        tt(T.over[:, lo:hi], T.stab[:].indirect(T.hu[:, lo // 16:hi // 16]), T.own[:, lo:hi], A.is_lt, ST + ["hu", "own%d" % q], OV[q][a:b])

    def most(k, a, b):
        op("v", lambda: V.transpose(T.kt[:, a:b], P[k][:, a:b]), ["#%d" % k], ["kt%d" % a])
        scan(T.ks[:, a:b], T.rst[:, a:b], T.kt[:, a:b], 0.0, A.mult, A.max, ["rst", "kt%d" % a], ["ks%d" % a])

    def compare_last():
        for h in range(2):
            mm(P[6 + h][:], IB, T.sgo[:, 512 * h:512 * h + 512], True, False, ["idb0", "sgo%d" % h], ["#%d" % (6 + h)])
            mm(P[6 + h][:], T.rot[:, 0:128], T.own[:, 3072 + 512 * h:3584 + 512 * h], False, True, ["rot0", "own3"], ["#%d" % (6 + h)])
        for h in range(2):
            act(T.over[:, 3072 + 512 * h:3584 + 512 * h], P[6 + h][:], F.Sign, ["#%d" % (6 + h), "EPS"], OV[3][h:h + 1], bias=EPS, scale=-1.0)

    def gather_s(h):
        act(T.sgo[:, 512 * h:512 * h + 512], T.stab[:].indirect(T.hu[:, 192 + 32 * h:224 + 32 * h]), F.Copy, ST + ["hu"], ["sgo%d" % h])

    def heights():
        for r in range(16):
            mm(P[4][:, 0:16], SEL[r], T.sg[:, r::16], r == 0, r == 15, ["sel", "sg"], ["#4"])

    for t in range(RO):
        d = 1 + t % (N - 1)
        dst, src = (rank + d) % N, (rank - d) % N
        ts(T.cu[:, 0:64], T.c[:, 0:64], 4096.0, A.min, ["c0", "CCOL"], ["cu0"], CCOL, A.max)
        gather_w(0)
        mm(P[6][:, 0:256], T.sh[:], T.c[:], True, True, ["sh"] + C, ["#6"])
        mm(P[7][:, 0:256], IDF, T.c[:], True, True, ["idf"] + C, ["#7"])
        ts(T.cu[:, 64:256], T.c[:, 64:256], 4096.0, A.min, ["c1", "CCOL"], ["cu1"], CCOL, A.max)
        if t == 0:
            consts_wide()
        ts(T.sg[:], T.c[:], 6000.0, A.is_ge, C, ["sg"])
        tt(T.ia[:], P[6][:, 0:256], T.c[:], A.mult, ["#6"] + C, ["ia"])
        ts(T.ib[:], T.ia[:], 5, A.arith_shift_right, ["ia"], ["ib"], 4095, A.bitwise_and)
        tt(T.fa[:], P[7][:, 0:256], T.ib[:], A.add, ["#7", "ib"], ["fa"])
        ts(T.hu[:], T.fa[:], HC[t], A.add, ["fa", "HC%d" % t], ["hu"], float(DEAD), A.min)
        if t > 0:
            lw = T.rload[:, 72 * (t - 1):72 * t]
            ts(T.d0[:, 1::16], lw.indirect(SL_U), 0.0625, A.mult, ["rl%d" % (t - 1), "slu"], ["d0", "d1"], -128.0, A.add,
               ext=[("al%d" % (t - 1), arrives((rank - 1 - (t - 1) % (N - 1)) % N))])
        mm(P[2][:, 0:256], ID13, T.c[:], True, False, ["id13"] + C, ["#2"])
        mm(P[3][:, 0:256], ID13, T.c[:], True, False, ["id13"] + C, ["#3"])
        mm(P[3][:, 0:256], IDF, T.ce[:], False, False, ["idf", "ce"], ["#3"])
        heights()
        if t == 0:
            consts_inv()
            strengths_up(0)
            strengths_up(1)
            gather_w(1)
            strengths_up(2)
            strengths_up(3)
            strengths(0)
            consts_tail()
            strengths(1)
            do_scan(0, t)
            strengths(2)
            strengths(3)
        else:
            gather_w(1)
            do_scan(0, t)
        mm(P[5][:, 0:256], T.topm[:], T.sg[:], True, True, ["topm", "sg"], ["#5"])
        gather_w(2)
        gather_w(3)
        compare(0)
        votes(0)
        gather_s(0)
        gather_s(1)
        do_scan(1, t)
        compare(1, 0, 1)
        do_scan(2, t)
        do_scan(3, t)
        compare(1, 1, 2)
        compare_last()
        votes(1)
        compare(2)
        votes(3)
        mm(P[7][:, 0:64], ID13, T.c[:, 128:192], True, False, ["id13"] + C, ["#7"])
        votes(2)
        most(0, 0, 128)
        most(0, 192, 256)
        for a, b in ((0, 128), (192, 256)):
            act(T.vb[:, a:b], P[0][:, a:b], F.Identity, ["#0", "NRHO"], ["vb%d" % a], scale=0.0625, bias=NRHO)
        ts(AN, P[4][:, 0:16], -0.0625, A.mult, ["#4"], ["an"], 17.0, A.add)
        most(1, 128, 192)
        act(T.vb[:, 128:192], P[1][:, 128:192], F.Identity, ["#1", "NRHO"], ["vb128"], scale=0.0625, bias=NRHO)
        KP = P[4][:, 96:112]
        for e in range(2):
            for b in range(2):
                j = 2 * e + b
                mm(P[4][:, 96 + e:112:2], T.sw[:, 128 * j:128 * j + 128], T.ks[:, 16 * b + 15::32], b == 0, b == 1,
                   ["sw%d" % j, "ks0", "ks128", "ks192"], ["#4"])
        if t == 0:
            ms(T.d0[:, 3072:4096], 30000.0, ["d1"])
        ts(MP, KP, 0.0625, A.mult, ["#4"], ["mp"], 128.0 - 15.0 / 32, A.add)
        ts(T9, KP, 144.0, A.is_ge, ["#4"], ["t9"])
        ts(KU, KP, 0.0, A.add, ["#4"], ["nu"])
        ts(KS, KP, -128.0, A.add, ["#4"], ["ks"])
        for a, b in ((0, 128), (192, 256)):
            mm(P[2][:, a:b], IB97, T.vb[:, a:b], False, False, ["idb1", "vb%d" % a], ["#2"])
            mm(P[2][:, a:b], IBV, T.vb[:, a:b], False, a > 0, ["idb2", "vb%d" % a], ["#2"])
        mm(P[1][:, 256:272], T.sumg[:], MP, True, False, ["sumg", "mp"], ["#1"])
        mm(P[1][:, 256:272], IB256, T9, False, True, ["idb3", "t9"], ["#1"])
        act(T.mm[:], T.mtab[:].indirect(KU), F.Copy, ["mtab", "nu"], ["mm"])
        act(T.pc[:], P[2][:, 0:256], F.Copy, ["#2"], ["pc"], bias=float(t))
        ts(RDY, P[1][:, 256:272], 1368.0, A.is_ge, ["#1"], ["rdy"])
        scan(CUM, RDY, RDY, 0.0, A.add, A.max, ["rdy"], ["cum"])
        mm(P[7][:, 0:64], IB97, T.vb[:, 128:192], False, False, ["idb1", "vb128"], ["#7"])
        mm(P[7][:, 0:64], IBV, T.vb[:, 128:192], False, True, ["idb2", "vb128"], ["#7"])
        mm(P[4][:, 64:80], IB, KS, True, False, ["idb0", "ks"], ["#4"])
        mm(P[4][:, 64:80], IBM16, MP, False, True, ["idb4", "mp"], ["#4"])
        mm(P[4][:, 48:64], IB, KS, True, False, ["idb0", "ks"], ["#4"])
        mm(P[4][:, 48:64], IBM16, MP, False, False, ["idb4", "mp"], ["#4"])
        mm(P[4][:, 48:64], T.t1[:, 128:256], RDY, False, False, ["t1b", "rdy"], ["#4"])
        mm(P[4][:, 48:64], T.bd[:, 128:256], CUM, False, True, ["bd1", "cum"], ["#4"])
        mm(P[4][:, 32:48], T.t1[:, 0:128], RDY, True, False, ["t1a", "rdy"], ["#4"])
        mm(P[4][:, 32:48], T.bd[:, 0:128], CUM, False, True, ["bd0", "cum"], ["#4"])
        act(T.pc[:, 128:192], P[7][:, 0:64], F.Copy, ["#7"], ["pc"], bias=float(t))
        act(T.top[:], P[5][:, 0:256], F.Relu, ["#5"], ["top"])
        mm(P[3][:, 0:256], IB97, T.vb[:], False, True, ["idb1", "vb0", "vb128", "vb192"], ["#3"])
        XO = 16 * 511 + 2176
        meta = T.smeta[:, 16 * t:16 * t + 16]
        tt(OF, P[4][:, 32:48], T.oc[:], A.min, ["#4", "oc"], ["of"])
        ts(meta, P[4][:, 48:64], float(XO), A.add, ["#4"], ["sm%d" % t], 1024.0, A.min)
        ts(OU, OF, 511.0, A.add, ["of"], ["ou"])
        send(dst, T.rmeta[:, 16 * t:16 * t + 16], meta, "am%d" % t, ["sm%d" % t])
        tt(T.cw[:].indirect(OU), T.pc[:], T.mm[:], A.add, ["ou", "pc", "mm"], ["cw"])
        ci = T.ci
        cp(ci[:, 0:64], T.cw[:, 0:64], ["cw"], ["ci0"])
        ts(ci[:, 64:128], ci[:, 0:64], 0x410FFF, A.bitwise_and, ["ci0"], ["ci1"])
        ts(ci[:, 128:192], ci[:, 0:64], 17, A.arith_shift_right, ["ci0"], ["ci2"], 31, A.bitwise_and)
        pay = T.spay[:, 64 * t:64 * t + 64]
        ts(pay, ci[:, 64:128], float(DEAD), A.min, ["ci1"], ["sp%d" % t], -2048.0, A.add)
        send(dst, T.rpay[:, 64 * t:64 * t + 64], pay, "ap%d" % t, ["sp%d" % t])
        ts(ci[:, 192:256], ci[:, 0:64], 0x41FFFF, A.bitwise_and, ["ci0"], ["ci3"])
        ts(T.cf[:], ci[:, 128:192], -97.0, A.mult, ["ci2"], ["cf"])
        ts(NS, P[4][:, 48:64], float(1024 - XO), A.is_ge, ["#4"], ["nsl"], 64.0, A.mult)
        tt(T.cf[:], T.cf[:], ci[:, 192:256], A.add, ["cf", "ci3"], ["cf"])
        tt(KB, NS, P[4][:, 64:80], A.subtract, ["nsl", "#4"], ["kb"])
        ts(ci[:, 128:192], T.cf[:], 1.0 / 13, A.mult, ["cf"], ["ci2"], 4096.0, A.min)
        ts(KB, KB, -2160.0, A.add, ["kb"], ["kb"])
        cp(T.lu[:], ci[:, 128:192], ["ci2"], ["lu"])
        act(T.lg[:], T.wtab[:].indirect(T.lu[:]), F.Copy, WT + ["lu"], ["lg"])
        tt(T.fb[:], P[3][:, 0:256], T.top[:], A.mult, ["#3", "top"], ["fb"])
        mm(P[5][:, 0:256], T.sh[:], T.fb[:], True, True, ["sh", "fb"], ["#5"])
        tt(NP, KB, AN, A.min, ["kb", "an"], ["np"])
        if t == 0:
            consts_land()
        if t == 1:
            consts_end()
        cp(NU, NP, ["np"], ["npu"])
        ts(N64, NP, 64.0, A.mult, ["np"], ["n64"])
        act(T.rsx[:], T.xtab[:].indirect(T.rmeta[:, 16 * t:16 * t + 16]), F.Copy, ["xtab", "xt2"], ["rsx"], ext=[("am%d" % t, arrives(src))])
        for r in range(1, 16):
            mm(P[0][:, 0:64], IB, T.lg[:, r::16], r == 1, r == 15, ["idb0", "lg"], ["#0"])
        sl = T.sload[:, 64 * t:64 * t + 64]
        act(sl, P[0][:, 0:64], F.Copy, ["#0"], ["sl%d" % t])
        send(dst, T.rload[:, 72 * t:72 * t + 64], sl, "al%d" % t, ["sl%d" % t])
        if t + 1 < RO:
            growth(t + 1)
        tt(T.ia[:], P[5][:, 0:256], T.pc[:], A.add, ["#5", "pc"], ["ia"])
        ts(T.ib[:], T.ia[:], 4095, A.bitwise_and, ["ia"], ["ib"])
        tt(T.loc[:], T.ktab[:].indirect(NU), T.ib[:], A.min, ["ktab", "npu", "ib"], ["loc"])
        tt(T.fc[:], T.rsx[:].indirect(T.rinv[:, 16 * d:16 * d + 16]), T.diag[:], A.mult, ["rsx", "diag"], ["fc"],
           ext=[("ainv", sum(arrives(q) for q in range(N) if q != rank))])
        scan(T.fa[:], T.rst[:], T.fc[:], 0.0, A.mult, A.add, ["rst", "fc"], ["fa"])
        tt(T.ti[:, 16:32], T.fa[:, 15::16], N64, A.add, ["fa", "n64"], ["ti1"])
        ts(T.ti[:, 32:48], T.ti[:, 16:32], 0x13FF, A.bitwise_and, ["ti1"], ["ti2"])
        ts(T.ti[:, 0:16], T.ti[:, 16:32], 0x103F, A.bitwise_and, ["ti1"], ["ti0"])
        ts(RO_U, T.ti[:, 32:48], 1024.0, A.min, ["ti2"], ["rou"])
        ts(SL_U, T.ti[:, 0:16], 64.0, A.min, ["ti0"], ["slu"])
        rp = T.rpay[:, 64 * t:64 * t + 64]
        for x in range(16):
            mm(P[6 + x // 8][:, 64 * (x % 8):64 * (x % 8) + 64], T.rot[:, 128 * x:128 * x + 128], rp, True, True, ["rot%d" % x], ["#%d" % (6 + x // 8)],
               ext=[("ap%d" % t, arrives(src))])
        act(T.rw[:, 0:512], P[6][:], F.Copy, ["#6"], ["rw0"], bias=-2048.0)
        ts(T.rw[:, 512:1024], P[7][:], -2048.0, A.add, ["#7"], ["rw1"])
        RW = ["rw0", "rw1", "rw2", "rou", "loc"]
        tt(T.comb[:, 0:64], T.rw[:].indirect(RO_U[:, 0:4]), T.loc[:, 0:64], A.max, RW, ["cb0"])
        tt(T.comb[:, 64:256], T.rw[:].indirect(RO_U[:, 4:16]), T.loc[:, 64:256], A.max, RW, ["cb1"])
        act(T.c[:, 0:64], T.comb[:, 0:64], F.Abs, ["cb0"], ["c0"])
        act(T.c[:, 64:256], T.comb[:, 64:256], F.Abs, ["cb1"], ["c1"])

    t = RO - 1
    op("v", lambda: V.transpose(T.fb[:], T.c[:]), C, ["fb"])
    mm(P[5][:, 0:256], IB256, T.c2k[:], True, False, ["idb3", "c2k"], ["#5"])
    ts(T.ha[:], T.fb[:].indirect(T.plu[:, 16:32]), -2048.0, A.add, ["fb", "plu1"], ["ha"])
    for b in range(2):
        for e in range(2):
            j = 2 * e + b
            mm(P[5][:, e:256:2], T.sw[:, 128 * j:128 * j + 128], T.ha[:, 128 * b:128 * b + 128], False, b == 1 and e == 1, ["sw%d" % j, "ha"], ["#5"])
    ts(T.sg[:], T.c[:], 6000.0, A.is_ge, C, ["sg"])
    heights()
    ts(T.fc[:], P[5][:, 0:256], 5000.0, A.is_ge, ["#5"], ["fc"], float(-DEAD - 1), A.mult)
    tt(T.ycs[:], P[5][:, 0:256], T.fc[:], A.add, ["#5", "fc"], ["ycs", "ycs2"])
    dma(T.yc[:], T.ycs[:], ["ycs"], [], "oc")
    cp(T.yis[:], T.rload[:, 72 * t:72 * t + 72].indirect(SL_U), ["rl%d" % t, "slu"], ["yis"],
       ext=[("al%d" % t, arrives((rank - 1 - t % (N - 1)) % N))])
    dma(T.yi[:], T.yis[:], ["yis"], [], "oi", "s")
    act(T.yns[:], P[4][:, 0:16], F.Copy, ["#4"], ["yns"], bias=16.0, scale=-0.0625)
    dma(T.yn[:], T.yns[:], ["yns"], [], "on", "s")

    count = emit(g, T, ops)
    for s in ("oc", "on", "oi"):
        g.sync.wait_ge(T.sem[s], count[s])
    g.wait_ge(T.sem.ls, sent[0])
